import numpy as np
import ml_dtypes


def mxq(x, axis, fmt="e4m3"):
    dtype, down = {"e4m3": (ml_dtypes.float8_e4m3fn, 7), "e5m2": (ml_dtypes.float8_e5m2, 14)}[fmt]
    v = np.moveaxis(np.asarray(x, np.float32).astype(ml_dtypes.bfloat16).astype(np.float64), axis, -1)
    blocks = v.reshape(v.shape[:-1] + (-1, 32))
    amax = np.abs(blocks).max(-1, keepdims=True)
    byte = np.maximum(np.where(amax > 0, np.frexp(amax)[1] - 1 + 127, 0) - down, 1)
    scale = np.exp2(byte - 127.0)
    codes = (blocks / scale).astype(np.float32).astype(dtype).astype(np.float64)
    return np.moveaxis((codes * scale).reshape(v.shape), -1, axis)


WIDE = False


def mx_kscale(k):
    if not WIDE:
        return np.ones(k)
    levels = np.array([10, -10, 5, -5, 0])
    if k % 512:
        return np.exp2(np.random.permutation(np.resize(levels, k // 32))).repeat(32)
    a = np.empty((k // 512, 16))
    for p in range(k // 512):
        a[p, :8] = np.random.permutation(np.resize(levels, 8))
        for g in range(8):
            far = levels[np.abs(levels - a[p, g]) >= 10]
            a[p, g + 8] = far[np.random.randint(len(far))]
    return np.exp2(a.ravel()).repeat(32)


def f64(x):
    return np.asarray(x).astype(np.float64)


def striped(idx):
    return np.tile(np.asarray(idx).reshape(-1, 16).T, (8, 1)).astype(np.uint16)


def unstriped(offs):
    return offs[:16].T.reshape(-1).astype(np.int64)


E2M1 = np.array([0.0, 0.5, 1.0, 1.5, 2.0, 3.0, 4.0, 6.0, -0.0, -0.5, -1.0, -1.5, -2.0, -3.0, -4.0, -6.0])


def pack_weight(w, fmt):
    k, n = w.shape
    w = f64(np.asarray(w, np.float32).astype(ml_dtypes.bfloat16)).reshape(k // 32, 32, n)
    amax = np.abs(w).max(1)
    if fmt == "e4m3":
        byte = np.frexp(amax)[1] - 1 + 127 - 7
    else:
        mant, ex = np.frexp(amax / 6.0)
        byte = np.where(mant > 0.5, ex, ex - 1) + 127
    byte = np.clip(np.where(amax > 0, byte, 1), 1, 254)
    scaled = (w * np.exp2(127.0 - byte)[:, None, :]).reshape(k, n).astype(np.float32)
    by_word = np.ascontiguousarray(scaled.reshape(k // 512, 128, 4, n).transpose(0, 1, 3, 2))
    if fmt == "e4m3":
        words = by_word.astype(ml_dtypes.float8_e4m3fn).view(np.uint8)
    else:
        c = by_word.astype(ml_dtypes.float4_e2m1fn).view(np.uint8) & 0xF
        words = (c[..., 0::2] | (c[..., 1::2] << 4)).reshape(k // 512, 128, 2 * n)
    return np.ascontiguousarray(words), np.ascontiguousarray(byte.astype(np.uint8).reshape(k // 512, 16, n))


def unpack_weight(words, scales, fmt):
    g, _, n = scales.shape
    words = np.ascontiguousarray(words).reshape(g, 128, n, -1)
    if fmt == "e4m3":
        vals = words.view(ml_dtypes.float8_e4m3fn).astype(np.float64)
    else:
        nib = np.empty((g, 128, n, 4), np.uint8)
        nib[..., 0::2] = words & 0xF
        nib[..., 1::2] = words >> 4
        vals = E2M1[nib]
    vals = vals * np.repeat(np.exp2(scales.astype(np.float64) - 127.0), 8, axis=1)[..., None]
    return vals.transpose(0, 1, 3, 2).reshape(g * 512, n)


def sigmoid(v):
    return 1.0 / (1.0 + np.exp(-v))


D, E, T, I, Q = 512, 512, 2048, 512, 128


def setup_inputs():
    n = np.random.standard_normal
    idx = np.random.permutation(T)[:I]
    fd = mx_kscale(D)
    fe = mx_kscale(E)
    keysp = pack_weight(n((D, T)) / fd[:, None], "e2m1")
    valsp = pack_weight(n((E, T)) / fe[:, None], "e2m1")
    return {
        "query": (n((D, Q)) * 0.8 / np.sqrt(D) * fd[:, None]).astype(np.float32),
        "keys_words": keysp[0],
        "keys_scales": keysp[1],
        "share": (np.random.uniform(0.2, 0.8, (Q, 1))).astype(np.float32),
        "gout": (n((E, Q)) * 1 / np.sqrt(E) * fe[:, None]).astype(np.float32),
        "vals_words": valsp[0],
        "vals_scales": valsp[1],
        "base": (0.5 * n((Q, I))).astype(np.float32),
        "offs": striped(idx),
    }


def reference(query, keys_words, keys_scales, share, gout, vals_words, vals_scales, base, offs):
    idx = unstriped(offs)
    keysu = unpack_weight(keys_words, keys_scales, "e2m1")
    valsu = unpack_weight(vals_words, vals_scales, "e2m1")
    queryq = mxq(f64(query), 0, "e4m3")
    keysidxg = keysu[:, idx]
    a = queryq.T @ keysidxg
    e0 = np.exp(a)
    s0 = sigmoid(a)
    p = e0 * f64(share) + s0 * (1.0 - f64(share)) * 3.0
    z = np.sum(p, axis=1, keepdims=True)
    goutq = mxq(f64(gout), 0, "e4m3")
    valsidxg = valsu[:, idx]
    c0 = goutq.T @ valsidxg
    dz = np.sum(c0 * p / np.square(z) * (-1.0), axis=1, keepdims=True)
    dp = c0 / z + dz
    ds0 = dp * 3.0 * (1.0 - f64(share))
    de0 = dp * f64(share)
    da = ds0 * s0 * (1.0 - s0) + de0 * e0
    hda = da * 512.0 * 2.0 * 512.0
    hde0 = hda * e0
    hds0 = hda * (1.0 - s0) * s0
    hdp = hde0 * f64(share) + hds0 * (1.0 - f64(share)) * 3.0
    hdz = np.sum(hdp, axis=1, keepdims=True)
    hz = np.sum(hdp * c0 / np.square(z) * (-1.0), axis=1, keepdims=True) + np.sum(hdz * (-1.0) * c0 * p / np.square(np.square(z)) * (-1.0), axis=1, keepdims=True) * z * 2.0
    hp = hdz * (-1.0) / np.square(z) * c0 + hz
    hs0 = hda * (1.0 - s0) * ds0 + hp * 3.0 * (1.0 - f64(share)) - hda * ds0 * s0
    he0 = hda * de0 + hp * f64(share)
    ha = hs0 * s0 * (1.0 - s0) + he0 * e0
    y = ha + f64(base)
    return y

@@ -1,0 +1,190 @@
+from contextlib import ExitStack
+
+import concourse.mybir as mybir
+
+F32 = mybir.dt.float32
+BF16 = mybir.dt.bfloat16
+I32 = mybir.dt.int32
+U32 = mybir.dt.uint32
+U16 = mybir.dt.uint16
+U8 = mybir.dt.uint8
+FP8X4 = mybir.dt.float8_e4m3fn_x4
+FP4X4 = mybir.dt.float4_e2m1fn_x4
+ACT = mybir.ActivationFunctionType
+ALU = mybir.AluOpType
+
+P = 128
+PACK = 4
+D, T, SLOTS, Q = 512, 2048, 512, 128
+HALF = SLOTS // 2
+PENALTY = 512.0 * 2.0 * 512.0
+
+FLOPS = 2 * 2 * D * Q * SLOTS
+
+
+def tile_attend_gpmixedparts_kernel(tc, query, keys_words, keys_scales, share, gout, vals_words, vals_scales, base, offs, out):
+    nc = tc.nc
+    halves = [slice(0, HALF), slice(HALF, SLOTS)]
+    list_halves = [slice(0, HALF // 16), slice(HALF // 16, SLOTS // 16)]
+
+    with ExitStack() as ctx:
+        keep = ctx.enter_context(tc.tile_pool(name="keep", bufs=1))
+        psum = ctx.enter_context(tc.psum_pool(name="psum", bufs=1))
+
+        def column(name):
+            return keep.tile([P, 1], F32, name=name)
+
+        def wide(name):
+            return keep.tile([P, SLOTS], F32, name=name)
+
+        offsets = keep.tile([P, SLOTS // 16], U16, name="offsets")
+        nc.sync.dma_start(offsets[:], offs)
+
+        k_bytes = keep.tile([P, T], U8, name="k_bytes", tag="kb", align_bytes=64)
+        v_bytes = keep.tile([P, T], U8, name="v_bytes")
+        nc.vector.memset(k_bytes[:].bitcast(I32), 0)
+        sums = keep.tile([P, 5], F32, name="sums")
+        nc.vector.memset(sums[:, 4:5], 1.0)
+        nc.vector.memset(v_bytes[:].bitcast(I32), 0)
+
+        k_words = keep.tile([P, T], U16, name="k_words")
+        nc.sync.dma_start(out=k_words[:].bitcast(I32), in_=keys_words[0].bitcast(I32))
+        q_raw = keep.tile([P, PACK, Q], F32, name="q_raw")
+        nc.sync.dma_start(out=q_raw[:], in_=query.rearrange("(p j) w -> p j w", j=PACK))
+        for quad in range(4):
+            nc.sync.dma_start(out=k_bytes[32 * quad : 32 * quad + 4, :].bitcast(I32),
+                                in_=keys_scales[0, 4 * quad : 4 * quad + 4, :].bitcast(I32))
+        share_sb = column("share_sb")
+        nc.gpsimd.dma_start(out=share_sb[:], in_=share)
+        g_raw = keep.tile([P, PACK, Q], F32, name="g_raw", tag="late")
+        nc.sync.dma_start(out=g_raw[:], in_=gout.rearrange("(p j) w -> p j w", j=PACK))
+        for quad in range(4):
+            nc.sync.dma_start(out=v_bytes[32 * quad : 32 * quad + 4, :].bitcast(I32),
+                              in_=vals_scales[0, 4 * quad : 4 * quad + 4, :].bitcast(I32))
+        v_words = keep.tile([P, T], U16, name="v_words", tag="vw")
+        nc.sync.dma_start(out=v_words[:].bitcast(I32), in_=vals_words[0].bitcast(I32))
+
+        warm = column("warm")
+        nc.scalar.activation(out=warm[:], in_=sums[:, 4:5], func=ACT.Exp)
+
+        gamma = column("gamma")
+        neg_gamma = column("neg_gamma")
+        weights = keep.tile([P, 5], F32, name="weights")
+        nc.gpsimd.tensor_scalar(gamma[:], share_sb[:], -0.75, 0.75, ALU.mult, ALU.add)
+        nc.gpsimd.tensor_scalar(neg_gamma[:], share_sb[:], 0.75, -0.75, ALU.mult, ALU.add)
+        nc.gpsimd.tensor_scalar(weights[:, 0:2], share_sb[:].to_broadcast([P, 2]), 1.0, 0.0, ALU.mult, ALU.add)
+        nc.gpsimd.tensor_scalar(weights[:, 2:4], share_sb[:].to_broadcast([P, 2]), -1.5, 1.5, ALU.mult, ALU.add)
+        nc.gpsimd.tensor_scalar(weights[:, 4:5], share_sb[:], -768.0, 768.0, ALU.mult, ALU.add)
+
+        def quantise(raw, name):
+            grouped = keep.tile([P, Q, PACK], BF16, name=name + "_grouped", align_bytes=64)
+            codes = keep.tile([P, Q], U32, name=name + "_codes", align_bytes=64)
+            scales = keep.tile([P, Q], U8, name=name + "_scales", align_bytes=64)
+            nc.scalar.copy(out=grouped[:], in_=raw[:].rearrange("p j w -> p w j"))
+            nc.vector.quantize_mx(out=codes[:].bitcast(FP8X4), scales=scales[:],
+                                  in_=grouped[:].rearrange("p w j -> p (w j)"))
+            return codes, scales
+
+        q_codes, q_scales = quantise(q_raw, "q")
+
+        kg_bytes = keep.tile([P, SLOTS], U8, name="kg_bytes", align_bytes=64)
+        kg_words = keep.tile([P, SLOTS], U16, name="kg_words", align_bytes=64)
+        nc.vector.tensor_copy(kg_words[:], k_words[:].indirect(offsets[:]))
+        scores = []
+        for i in range(2):
+            nc.vector.tensor_copy(kg_bytes[:, halves[i]], k_bytes[:].indirect(offsets[:, list_halves[i]]))
+            bank = psum.tile([P, HALF], F32, name="score%d" % i)
+            nc.tensor.matmul_mx(out=bank[:], lhsT=q_codes[:].bitcast(FP8X4), lhsT_scale=q_scales[:],
+                                rhs=kg_words[:, halves[i]].bitcast(FP4X4), rhs_scale=kg_bytes[:, halves[i]],
+                                start=True, stop=True)
+            scores.append(bank)
+
+        g_codes, g_scales = quantise(g_raw, "g")
+        base_sb = keep.tile([P, SLOTS], F32, name="base_sb", tag="late")
+        nc.sync.dma_start(out=base_sb[:], in_=base)
+
+        vg_bytes = keep.tile([P, SLOTS], U8, name="vg_bytes", tag="kb", align_bytes=64)
+        nc.vector.tensor_copy(vg_bytes[:], v_bytes[:].indirect(offsets[:]))
+        vg_words = keep.tile([P, SLOTS], U16, name="vg_words", align_bytes=64)
+        c = psum.tile([P, SLOTS], F32, name="c")
+        for i in range(2):
+            nc.vector.tensor_copy(vg_words[:, halves[i]], v_words[:].indirect(offsets[:, list_halves[i]]))
+            nc.tensor.matmul_mx(out=c[:, halves[i]], lhsT=g_codes[:].bitcast(FP8X4), lhsT_scale=g_scales[:],
+                                rhs=vg_words[:, halves[i]].bitcast(FP4X4), rhs_scale=vg_bytes[:, halves[i]],
+                                start=True, stop=True)
+
+        t = wide("t")
+        e = wide("e")
+        t2 = wide("t2")
+        y = wide("y")
+        r2 = wide("r2")
+        for i in range(2):
+            cols = halves[i]
+            nc.scalar.activation(out=t[:, cols], in_=scores[i][:], func=ACT.Tanh, scale=0.5, accum_out=sums[:, 2 + i : 3 + i])
+            nc.scalar.activation(out=e[:, cols], in_=scores[i][:], func=ACT.Exp, accum_out=sums[:, i : i + 1])
+        for cols in halves:
+            nc.scalar.activation(out=t2[:, cols], in_=t[:, cols], func=ACT.Square)
+        for cols in halves:
+            nc.scalar.activation(out=y[:, cols], in_=t2[:, cols], func=ACT.Identity, scale=neg_gamma[:], bias=gamma[:])
+        nc.scalar.activation(out=r2[:], in_=t[:], func=ACT.Square, bias=1.0)
+
+        z = column("z")
+        rz = column("rz")
+        reuse = keep.tile([P, 2 * SLOTS + 8], F32, name="reuse", tag="vw")
+        g = reuse[:, 0:SLOTS]
+        d = reuse[:, SLOTS : 2 * SLOTS]
+        terms = reuse[:, 2 * SLOTS : 2 * SLOTS + 5]
+        nc.vector.scalar_tensor_tensor(terms, sums[:], 1.0, weights[:], ALU.mult, ALU.mult, accum_out=z[:])
+        nc.vector.reciprocal(rz[:], z[:])
+        for cols in halves:
+            nc.vector.scalar_tensor_tensor(g[:, cols], e[:, cols], share_sb[:], y[:, cols], ALU.mult, ALU.add)
+
+        parts = keep.tile([P, 2], F32, name="parts")
+        c_g = wide("c_g")
+        nc.vector.scalar_tensor_tensor(c_g[:], c[:], -1.0, g, ALU.mult, ALU.mult, accum_out=parts[:, 1:2])
+        c_r2 = wide("c_r2")
+        nc.vector.scalar_tensor_tensor(c_r2[:], c[:], neg_gamma[:], r2[:], ALU.mult, ALU.mult, accum_out=parts[:, 0:1])
+
+        g2 = wide("g2")
+        m0 = column("m0")
+        nc.scalar.activation(out=g2[:], in_=g, func=ACT.Square, scale=rz[:], accum_out=m0[:])
+        c_g2 = wide("c_g2")
+        m1 = column("m1")
+        nc.vector.scalar_tensor_tensor(c_g2[:], c[:], 1.0, g2[:], ALU.mult, ALU.mult, accum_out=m1[:])
+        c2_g2 = wide("c2_g2")
+        m2 = column("m2")
+        nc.scalar.activation(out=c2_g2[:], in_=c_g[:], func=ACT.Square, scale=rz[:], accum_out=m2[:])
+        neg_m = column("neg_m")
+        parts_rz = keep.tile([P, 2], F32, name="parts_rz")
+        nc.scalar.activation(out=parts_rz[:], in_=parts[:], func=ACT.Identity, scale=rz[:], accum_out=neg_m[:])
+        u = wide("u")
+        nc.scalar.activation(out=u[:], in_=c[:], func=ACT.Identity, bias=neg_m[:])
+
+        h = wide("h")
+        for cols in halves:
+            nc.vector.scalar_tensor_tensor(d[:, cols], t[:, cols], 1.0, r2[:, cols], ALU.subtract, ALU.mult)
+        for cols in halves:
+            nc.vector.scalar_tensor_tensor(h[:, cols], d[:, cols], gamma[:], g[:, cols], ALU.mult, ALU.add)
+
+        sum_a = column("sum_a")
+        nc.scalar.activation(out=sum_a[:], in_=m0[:], func=ACT.Identity, scale=neg_m[:], bias=m1[:])
+        inner = column("inner")
+        nc.scalar.activation(out=inner[:], in_=sum_a[:], func=ACT.Identity, bias=m1[:])
+        sum_b = column("sum_b")
+        nc.scalar.activation(out=sum_b[:], in_=inner[:], func=ACT.Identity, scale=neg_m[:], bias=m2[:])
+        k_rz = column("k_rz")
+        nc.scalar.mul(k_rz[:], rz[:], PENALTY)
+
+        x1 = wide("x1")
+        x2 = wide("x2")
+        x3 = wide("x3")
+        result = wide("result")
+        for cols in halves:
+            nc.vector.scalar_tensor_tensor(x1[:, cols], u[:, cols], rz[:], h[:, cols], ALU.mult, ALU.mult)
+        for cols in halves:
+            nc.vector.scalar_tensor_tensor(x2[:, cols], x1[:, cols], sum_a[:], u[:, cols], ALU.subtract, ALU.mult)
+        for cols in halves:
+            nc.vector.scalar_tensor_tensor(x3[:, cols], x2[:, cols], sum_b[:], g[:, cols], ALU.subtract, ALU.mult)
+        for cols, queue in zip(halves, (nc.sync, nc.scalar)):
+            nc.vector.scalar_tensor_tensor(result[:, cols], x3[:, cols], k_rz[:], base_sb[:, cols], ALU.mult, ALU.add)
+            queue.dma_start(out=out[:, cols], in_=result[:, cols])

@@ -40,32 +40,31 @@ def tile_attend_gpmixedparts_kernel(tc, query, keys_words, keys_scales, share, g
         offsets = keep.tile([P, SLOTS // 16], U16, name="offsets")
         nc.sync.dma_start(offsets[:], offs)
 
-        k_bytes = keep.tile([P, T], U8, name="k_bytes", tag="kb", align_bytes=64)
+        share_sb = column("share_sb")
+        nc.scalar.dma_start(out=share_sb[:], in_=share)
+        zero = keep.tile([P, 1], F32, name="zero")
+        nc.gpsimd.memset(zero[:], 0.0)
+        k_bytes = keep.tile([P, T], U8, name="k_bytes")
         v_bytes = keep.tile([P, T], U8, name="v_bytes")
         nc.vector.memset(k_bytes[:].bitcast(I32), 0)
         sums = keep.tile([P, 5], F32, name="sums")
-        nc.vector.memset(sums[:, 4:5], 1.0)
+        nc.scalar.activation(out=sums[:, 4:5], in_=zero[:], func=ACT.Exp)
         nc.vector.memset(v_bytes[:].bitcast(I32), 0)
 
-        k_words = keep.tile([P, T], U16, name="k_words")
-        nc.sync.dma_start(out=k_words[:].bitcast(I32), in_=keys_words[0].bitcast(I32))
-        q_raw = keep.tile([P, PACK, Q], F32, name="q_raw")
+        q_raw = keep.tile([P, PACK, Q], F32, name="q_raw", tag="q_raw")
         nc.sync.dma_start(out=q_raw[:], in_=query.rearrange("(p j) w -> p j w", j=PACK))
         for quad in range(4):
             nc.sync.dma_start(out=k_bytes[32 * quad : 32 * quad + 4, :].bitcast(I32),
                                 in_=keys_scales[0, 4 * quad : 4 * quad + 4, :].bitcast(I32))
-        share_sb = column("share_sb")
-        nc.gpsimd.dma_start(out=share_sb[:], in_=share)
-        g_raw = keep.tile([P, PACK, Q], F32, name="g_raw", tag="late")
+        k_words = keep.tile([P, T], U16, name="k_words")
+        nc.sync.dma_start(out=k_words[:].bitcast(I32), in_=keys_words[0].bitcast(I32))
+        g_raw = keep.tile([P, PACK, Q], F32, name="g_raw", tag="g_raw")
         nc.sync.dma_start(out=g_raw[:], in_=gout.rearrange("(p j) w -> p j w", j=PACK))
         for quad in range(4):
             nc.sync.dma_start(out=v_bytes[32 * quad : 32 * quad + 4, :].bitcast(I32),
                               in_=vals_scales[0, 4 * quad : 4 * quad + 4, :].bitcast(I32))
         v_words = keep.tile([P, T], U16, name="v_words", tag="vw")
         nc.sync.dma_start(out=v_words[:].bitcast(I32), in_=vals_words[0].bitcast(I32))
-
-        warm = column("warm")
-        nc.scalar.activation(out=warm[:], in_=sums[:, 4:5], func=ACT.Exp)
 
         gamma = column("gamma")
         neg_gamma = column("neg_gamma")
@@ -76,44 +75,43 @@ def tile_attend_gpmixedparts_kernel(tc, query, keys_words, keys_scales, share, g
         nc.gpsimd.tensor_scalar(weights[:, 2:4], share_sb[:].to_broadcast([P, 2]), -1.5, 1.5, ALU.mult, ALU.add)
         nc.gpsimd.tensor_scalar(weights[:, 4:5], share_sb[:], -768.0, 768.0, ALU.mult, ALU.add)
 
-        def quantise(raw, name):
+        def quantise(raw, name, interleave):
             grouped = keep.tile([P, Q, PACK], BF16, name=name + "_grouped", align_bytes=64)
             codes = keep.tile([P, Q], U32, name=name + "_codes", align_bytes=64)
             scales = keep.tile([P, Q], U8, name=name + "_scales", align_bytes=64)
-            nc.scalar.copy(out=grouped[:], in_=raw[:].rearrange("p j w -> p w j"))
+            interleave(out=grouped[:], in_=raw[:].rearrange("p j w -> p w j"))
             nc.vector.quantize_mx(out=codes[:].bitcast(FP8X4), scales=scales[:],
                                   in_=grouped[:].rearrange("p w j -> p (w j)"))
             return codes, scales
 
-        q_codes, q_scales = quantise(q_raw, "q")
-
+        q_codes, q_scales = quantise(q_raw, "q", nc.vector.tensor_copy)
         kg_bytes = keep.tile([P, SLOTS], U8, name="kg_bytes", align_bytes=64)
-        kg_words = keep.tile([P, SLOTS], U16, name="kg_words", align_bytes=64)
-        nc.vector.tensor_copy(kg_words[:], k_words[:].indirect(offsets[:]))
+        nc.vector.tensor_copy(kg_bytes[:], k_bytes[:].indirect(offsets[:]))
+        kg_words = [keep.tile([P, HALF], U16, name="kg_words%d" % i, align_bytes=64) for i in range(2)]
         scores = []
         for i in range(2):
-            nc.vector.tensor_copy(kg_bytes[:, halves[i]], k_bytes[:].indirect(offsets[:, list_halves[i]]))
+            nc.vector.tensor_copy(kg_words[i][:], k_words[:].indirect(offsets[:, list_halves[i]]))
             bank = psum.tile([P, HALF], F32, name="score%d" % i)
             nc.tensor.matmul_mx(out=bank[:], lhsT=q_codes[:].bitcast(FP8X4), lhsT_scale=q_scales[:],
-                                rhs=kg_words[:, halves[i]].bitcast(FP4X4), rhs_scale=kg_bytes[:, halves[i]],
+                                rhs=kg_words[i][:].bitcast(FP4X4), rhs_scale=kg_bytes[:, halves[i]],
                                 start=True, stop=True)
             scores.append(bank)
 
-        g_codes, g_scales = quantise(g_raw, "g")
-        base_sb = keep.tile([P, SLOTS], F32, name="base_sb", tag="late")
+        g_codes, g_scales = quantise(g_raw, "g", nc.scalar.copy)
+        base_sb = keep.tile([P, SLOTS], F32, name="base_sb", tag="q_raw")
         nc.sync.dma_start(out=base_sb[:], in_=base)
 
-        vg_bytes = keep.tile([P, SLOTS], U8, name="vg_bytes", tag="kb", align_bytes=64)
+        vg_bytes = keep.tile([P, SLOTS], U8, name="vg_bytes", align_bytes=64)
         nc.vector.tensor_copy(vg_bytes[:], v_bytes[:].indirect(offsets[:]))
-        vg_words = keep.tile([P, SLOTS], U16, name="vg_words", align_bytes=64)
+        vg_words = [keep.tile([P, HALF], U16, name="vg_words%d" % i, align_bytes=64) for i in range(2)]
         c = psum.tile([P, SLOTS], F32, name="c")
         for i in range(2):
-            nc.vector.tensor_copy(vg_words[:, halves[i]], v_words[:].indirect(offsets[:, list_halves[i]]))
+            nc.vector.tensor_copy(vg_words[i][:], v_words[:].indirect(offsets[:, list_halves[i]]))
             nc.tensor.matmul_mx(out=c[:, halves[i]], lhsT=g_codes[:].bitcast(FP8X4), lhsT_scale=g_scales[:],
-                                rhs=vg_words[:, halves[i]].bitcast(FP4X4), rhs_scale=vg_bytes[:, halves[i]],
+                                rhs=vg_words[i][:].bitcast(FP4X4), rhs_scale=vg_bytes[:, halves[i]],
                                 start=True, stop=True)
 
-        t = wide("t")
+        t = keep.tile([P, SLOTS], F32, name="t", tag="g_raw")
         e = wide("e")
         t2 = wide("t2")
         y = wide("y")

@@ -104,10 +104,10 @@ def tile_attend_gpmixedparts_kernel(tc, query, keys_words, keys_scales, share, g
         vg_bytes = keep.tile([P, SLOTS], U8, name="vg_bytes", align_bytes=64)
         nc.vector.tensor_copy(vg_bytes[:], v_bytes[:].indirect(offsets[:]))
         vg_words = [keep.tile([P, HALF], U16, name="vg_words%d" % i, align_bytes=64) for i in range(2)]
-        c = psum.tile([P, SLOTS], F32, name="c")
+        c = [psum.tile([P, HALF], F32, name="c%d" % i) for i in range(2)]
         for i in range(2):
             nc.vector.tensor_copy(vg_words[i][:], v_words[:].indirect(offsets[:, list_halves[i]]))
-            nc.tensor.matmul_mx(out=c[:, halves[i]], lhsT=g_codes[:].bitcast(FP8X4), lhsT_scale=g_scales[:],
+            nc.tensor.matmul_mx(out=c[i][:], lhsT=g_codes[:].bitcast(FP8X4), lhsT_scale=g_scales[:],
                                 rhs=vg_words[i][:].bitcast(FP4X4), rhs_scale=vg_bytes[:, halves[i]],
                                 start=True, stop=True)
 
@@ -133,45 +133,50 @@ def tile_attend_gpmixedparts_kernel(tc, query, keys_words, keys_scales, share, g
         d = reuse[:, SLOTS : 2 * SLOTS]
         terms = reuse[:, 2 * SLOTS : 2 * SLOTS + 5]
         nc.vector.scalar_tensor_tensor(terms, sums[:], 1.0, weights[:], ALU.mult, ALU.mult, accum_out=z[:])
+        nc.vector.scalar_tensor_tensor(g[:, halves[0]], e[:, halves[0]], share_sb[:], y[:, halves[0]], ALU.mult, ALU.add)
         nc.vector.reciprocal(rz[:], z[:])
-        for cols in halves:
-            nc.vector.scalar_tensor_tensor(g[:, cols], e[:, cols], share_sb[:], y[:, cols], ALU.mult, ALU.add)
+        nc.vector.scalar_tensor_tensor(d[:, halves[0]], t[:, halves[0]], 1.0, y[:, halves[0]], ALU.add, ALU.mult)
+        nc.vector.scalar_tensor_tensor(g[:, halves[1]], e[:, halves[1]], share_sb[:], y[:, halves[1]], ALU.mult, ALU.add)
+        nc.vector.scalar_tensor_tensor(d[:, halves[1]], t[:, halves[1]], 1.0, y[:, halves[1]], ALU.add, ALU.mult)
+        h = wide("h")
+        nc.gpsimd.tensor_tensor(h[:], g, d, ALU.subtract)
 
-        parts = keep.tile([P, 2], F32, name="parts")
+        parts = keep.tile([P, 4], F32, name="parts")
         c_g = wide("c_g")
-        nc.vector.scalar_tensor_tensor(c_g[:], c[:], -1.0, g, ALU.mult, ALU.mult, accum_out=parts[:, 1:2])
         c_r2 = wide("c_r2")
-        nc.vector.scalar_tensor_tensor(c_r2[:], c[:], neg_gamma[:], r2[:], ALU.mult, ALU.mult, accum_out=parts[:, 0:1])
+        for i, cols in enumerate(halves):
+            nc.vector.scalar_tensor_tensor(c_g[:, cols], c[i][:], -1.0, g[:, cols], ALU.mult, ALU.mult, accum_out=parts[:, i : i + 1])
+        for i, cols in enumerate(halves):
+            nc.vector.scalar_tensor_tensor(c_r2[:, cols], c[i][:], neg_gamma[:], r2[:, cols], ALU.mult, ALU.mult, accum_out=parts[:, 2 + i : 3 + i])
 
         g2 = wide("g2")
         m0 = column("m0")
         nc.scalar.activation(out=g2[:], in_=g, func=ACT.Square, scale=rz[:], accum_out=m0[:])
         c_g2 = wide("c_g2")
-        m1 = column("m1")
-        nc.vector.scalar_tensor_tensor(c_g2[:], c[:], 1.0, g2[:], ALU.mult, ALU.mult, accum_out=m1[:])
+        a_terms = keep.tile([P, 3], F32, name="a_terms")
+        for i, cols in enumerate(halves):
+            nc.vector.scalar_tensor_tensor(c_g2[:, cols], c[i][:], 1.0, g2[:, cols], ALU.mult, ALU.mult, accum_out=a_terms[:, i : i + 1])
+        k_rz = column("k_rz")
+        nc.scalar.mul(k_rz[:], rz[:], PENALTY)
         c2_g2 = wide("c2_g2")
         m2 = column("m2")
         nc.scalar.activation(out=c2_g2[:], in_=c_g[:], func=ACT.Square, scale=rz[:], accum_out=m2[:])
         neg_m = column("neg_m")
-        parts_rz = keep.tile([P, 2], F32, name="parts_rz")
+        parts_rz = keep.tile([P, 4], F32, name="parts_rz")
         nc.scalar.activation(out=parts_rz[:], in_=parts[:], func=ACT.Identity, scale=rz[:], accum_out=neg_m[:])
         u = wide("u")
-        nc.scalar.activation(out=u[:], in_=c[:], func=ACT.Identity, bias=neg_m[:])
-
-        h = wide("h")
-        for cols in halves:
-            nc.vector.scalar_tensor_tensor(d[:, cols], t[:, cols], 1.0, r2[:, cols], ALU.subtract, ALU.mult)
-        for cols in halves:
-            nc.vector.scalar_tensor_tensor(h[:, cols], d[:, cols], gamma[:], g[:, cols], ALU.mult, ALU.add)
-
+        nc.scalar.activation(out=u[:, halves[0]], in_=c[0][:], func=ACT.Identity, bias=neg_m[:])
+        nc.scalar.activation(out=a_terms[:, 2:3], in_=m0[:], func=ACT.Identity, scale=neg_m[:])
+        nc.scalar.activation(out=u[:, halves[1]], in_=c[1][:], func=ACT.Identity, bias=neg_m[:])
         sum_a = column("sum_a")
-        nc.scalar.activation(out=sum_a[:], in_=m0[:], func=ACT.Identity, scale=neg_m[:], bias=m1[:])
+        a_copy = keep.tile([P, 3], F32, name="a_copy")
+        nc.scalar.activation(out=a_copy[:], in_=a_terms[:], func=ACT.Identity, accum_out=sum_a[:])
+        m_m0 = column("m_m0")
+        nc.scalar.mul(m_m0[:], a_terms[:, 2:3], -1.0)
         inner = column("inner")
-        nc.scalar.activation(out=inner[:], in_=sum_a[:], func=ACT.Identity, bias=m1[:])
+        nc.scalar.activation(out=inner[:], in_=sum_a[:], func=ACT.Identity, scale=2.0, bias=m_m0[:])
         sum_b = column("sum_b")
         nc.scalar.activation(out=sum_b[:], in_=inner[:], func=ACT.Identity, scale=neg_m[:], bias=m2[:])
-        k_rz = column("k_rz")
-        nc.scalar.mul(k_rz[:], rz[:], PENALTY)
 
         x1 = wide("x1")
         x2 = wide("x2")

@@ -45,7 +45,7 @@ def tile_attend_gpmixedparts_kernel(tc, query, keys_words, keys_scales, share, g
         zero = keep.tile([P, 1], F32, name="zero")
         nc.gpsimd.memset(zero[:], 0.0)
         k_bytes = keep.tile([P, T], U8, name="k_bytes")
-        v_bytes = keep.tile([P, T], U8, name="v_bytes")
+        v_bytes = keep.tile([P, T], U8, name="v_bytes", tag="vb")
         nc.vector.memset(k_bytes[:].bitcast(I32), 0)
         sums = keep.tile([P, 5], F32, name="sums")
         nc.scalar.activation(out=sums[:, 4:5], in_=zero[:], func=ACT.Exp)
@@ -60,11 +60,11 @@ def tile_attend_gpmixedparts_kernel(tc, query, keys_words, keys_scales, share, g
         nc.sync.dma_start(out=k_words[:].bitcast(I32), in_=keys_words[0].bitcast(I32))
         g_raw = keep.tile([P, PACK, Q], F32, name="g_raw", tag="g_raw")
         nc.sync.dma_start(out=g_raw[:], in_=gout.rearrange("(p j) w -> p j w", j=PACK))
+        v_words = keep.tile([P, T], U16, name="v_words")
+        nc.sync.dma_start(out=v_words[:].bitcast(I32), in_=vals_words[0].bitcast(I32))
         for quad in range(4):
             nc.sync.dma_start(out=v_bytes[32 * quad : 32 * quad + 4, :].bitcast(I32),
                               in_=vals_scales[0, 4 * quad : 4 * quad + 4, :].bitcast(I32))
-        v_words = keep.tile([P, T], U16, name="v_words", tag="vw")
-        nc.sync.dma_start(out=v_words[:].bitcast(I32), in_=vals_words[0].bitcast(I32))
 
         gamma = column("gamma")
         neg_gamma = column("neg_gamma")
@@ -101,14 +101,14 @@ def tile_attend_gpmixedparts_kernel(tc, query, keys_words, keys_scales, share, g
         base_sb = keep.tile([P, SLOTS], F32, name="base_sb", tag="q_raw")
         nc.sync.dma_start(out=base_sb[:], in_=base)
 
-        vg_bytes = keep.tile([P, SLOTS], U8, name="vg_bytes", align_bytes=64)
-        nc.vector.tensor_copy(vg_bytes[:], v_bytes[:].indirect(offsets[:]))
-        vg_words = [keep.tile([P, HALF], U16, name="vg_words%d" % i, align_bytes=64) for i in range(2)]
+        vg_words = keep.tile([P, SLOTS], U16, name="vg_words", align_bytes=64)
+        nc.vector.tensor_copy(vg_words[:], v_words[:].indirect(offsets[:]))
+        vg_bytes = [keep.tile([P, HALF], U8, name="vg_bytes%d" % i, align_bytes=64) for i in range(2)]
         c = [psum.tile([P, HALF], F32, name="c%d" % i) for i in range(2)]
         for i in range(2):
-            nc.vector.tensor_copy(vg_words[i][:], v_words[:].indirect(offsets[:, list_halves[i]]))
+            nc.vector.tensor_copy(vg_bytes[i][:], v_bytes[:].indirect(offsets[:, list_halves[i]]))
             nc.tensor.matmul_mx(out=c[i][:], lhsT=g_codes[:].bitcast(FP8X4), lhsT_scale=g_scales[:],
-                                rhs=vg_words[i][:].bitcast(FP4X4), rhs_scale=vg_bytes[:, halves[i]],
+                                rhs=vg_words[:, halves[i]].bitcast(FP4X4), rhs_scale=vg_bytes[i][:],
                                 start=True, stop=True)
 
         t = keep.tile([P, SLOTS], F32, name="t", tag="g_raw")
@@ -128,7 +128,7 @@ def tile_attend_gpmixedparts_kernel(tc, query, keys_words, keys_scales, share, g
 
         z = column("z")
         rz = column("rz")
-        reuse = keep.tile([P, 2 * SLOTS + 8], F32, name="reuse", tag="vw")
+        reuse = keep.tile([P, 2 * SLOTS + 8], F32, name="reuse", tag="vb")
         g = reuse[:, 0:SLOTS]
         d = reuse[:, SLOTS : 2 * SLOTS]
         terms = reuse[:, 2 * SLOTS : 2 * SLOTS + 5]

from contextlib import ExitStack

import concourse.mybir as mybir

F32 = mybir.dt.float32
BF16 = mybir.dt.bfloat16
I32 = mybir.dt.int32
U32 = mybir.dt.uint32
U16 = mybir.dt.uint16
U8 = mybir.dt.uint8
FP8X4 = mybir.dt.float8_e4m3fn_x4
FP4X4 = mybir.dt.float4_e2m1fn_x4
ACT = mybir.ActivationFunctionType
ALU = mybir.AluOpType

P = 128
PACK = 4
D, T, SLOTS, Q = 512, 2048, 512, 128
HALF = SLOTS // 2
PENALTY = 512.0 * 2.0 * 512.0

FLOPS = 2 * 2 * D * Q * SLOTS


def tile_attend_gpmixedparts_kernel(tc, query, keys_words, keys_scales, share, gout, vals_words, vals_scales, base, offs, out):
    nc = tc.nc
    halves = [slice(0, HALF), slice(HALF, SLOTS)]
    list_halves = [slice(0, HALF // 16), slice(HALF // 16, SLOTS // 16)]

    with ExitStack() as ctx:
        keep = ctx.enter_context(tc.tile_pool(name="keep", bufs=1))
        psum = ctx.enter_context(tc.psum_pool(name="psum", bufs=1))

        def column(name):
            return keep.tile([P, 1], F32, name=name)

        def wide(name):
            return keep.tile([P, SLOTS], F32, name=name)

        offsets = keep.tile([P, SLOTS // 16], U16, name="offsets")
        nc.sync.dma_start(offsets[:], offs)

        share_sb = column("share_sb")
        nc.scalar.dma_start(out=share_sb[:], in_=share)
        zero = keep.tile([P, 1], F32, name="zero")
        nc.gpsimd.memset(zero[:], 0.0)
        k_bytes = keep.tile([P, T], U8, name="k_bytes")
        v_bytes = keep.tile([P, T], U8, name="v_bytes", tag="vb")
        nc.vector.memset(k_bytes[:].bitcast(I32), 0)
        sums = keep.tile([P, 5], F32, name="sums")
        nc.scalar.activation(out=sums[:, 4:5], in_=zero[:], func=ACT.Exp)
        nc.vector.memset(v_bytes[:].bitcast(I32), 0)

        q_raw = keep.tile([P, PACK, Q], F32, name="q_raw", tag="q_raw")
        nc.sync.dma_start(out=q_raw[:], in_=query.rearrange("(p j) w -> p j w", j=PACK))
        for quad in range(4):
            nc.sync.dma_start(out=k_bytes[32 * quad : 32 * quad + 4, :].bitcast(I32),
                                in_=keys_scales[0, 4 * quad : 4 * quad + 4, :].bitcast(I32))
        k_words = keep.tile([P, T], U16, name="k_words")
        nc.sync.dma_start(out=k_words[:].bitcast(I32), in_=keys_words[0].bitcast(I32))
        g_raw = keep.tile([P, PACK, Q], F32, name="g_raw", tag="g_raw")
        nc.sync.dma_start(out=g_raw[:], in_=gout.rearrange("(p j) w -> p j w", j=PACK))
        v_words = keep.tile([P, T], U16, name="v_words")
        nc.sync.dma_start(out=v_words[:].bitcast(I32), in_=vals_words[0].bitcast(I32))
        for quad in range(4):
            nc.sync.dma_start(out=v_bytes[32 * quad : 32 * quad + 4, :].bitcast(I32),
                              in_=vals_scales[0, 4 * quad : 4 * quad + 4, :].bitcast(I32))

        gamma = column("gamma")
        neg_gamma = column("neg_gamma")
        weights = keep.tile([P, 5], F32, name="weights")
        nc.gpsimd.tensor_scalar(gamma[:], share_sb[:], -0.75, 0.75, ALU.mult, ALU.add)
        nc.gpsimd.tensor_scalar(neg_gamma[:], share_sb[:], 0.75, -0.75, ALU.mult, ALU.add)
        nc.gpsimd.tensor_scalar(weights[:, 0:2], share_sb[:].to_broadcast([P, 2]), 1.0, 0.0, ALU.mult, ALU.add)
        nc.gpsimd.tensor_scalar(weights[:, 2:4], share_sb[:].to_broadcast([P, 2]), -1.5, 1.5, ALU.mult, ALU.add)
        nc.gpsimd.tensor_scalar(weights[:, 4:5], share_sb[:], -768.0, 768.0, ALU.mult, ALU.add)

        def quantise(raw, name, interleave):
            grouped = keep.tile([P, Q, PACK], BF16, name=name + "_grouped", align_bytes=64)
            codes = keep.tile([P, Q], U32, name=name + "_codes", align_bytes=64)
            scales = keep.tile([P, Q], U8, name=name + "_scales", align_bytes=64)
            interleave(out=grouped[:], in_=raw[:].rearrange("p j w -> p w j"))
            nc.vector.quantize_mx(out=codes[:].bitcast(FP8X4), scales=scales[:],
                                  in_=grouped[:].rearrange("p w j -> p (w j)"))
            return codes, scales

        q_codes, q_scales = quantise(q_raw, "q", nc.vector.tensor_copy)
        kg_bytes = keep.tile([P, SLOTS], U8, name="kg_bytes", align_bytes=64)
        nc.vector.tensor_copy(kg_bytes[:], k_bytes[:].indirect(offsets[:]))
        kg_words = [keep.tile([P, HALF], U16, name="kg_words%d" % i, align_bytes=64) for i in range(2)]
        scores = []
        for i in range(2):
            nc.vector.tensor_copy(kg_words[i][:], k_words[:].indirect(offsets[:, list_halves[i]]))
            bank = psum.tile([P, HALF], F32, name="score%d" % i)
            nc.tensor.matmul_mx(out=bank[:], lhsT=q_codes[:].bitcast(FP8X4), lhsT_scale=q_scales[:],
                                rhs=kg_words[i][:].bitcast(FP4X4), rhs_scale=kg_bytes[:, halves[i]],
                                start=True, stop=True)
            scores.append(bank)

        g_codes, g_scales = quantise(g_raw, "g", nc.scalar.copy)
        base_sb = keep.tile([P, SLOTS], F32, name="base_sb", tag="q_raw")
        nc.sync.dma_start(out=base_sb[:], in_=base)

        vg_words = keep.tile([P, SLOTS], U16, name="vg_words", align_bytes=64)
        nc.vector.tensor_copy(vg_words[:], v_words[:].indirect(offsets[:]))
        vg_bytes = [keep.tile([P, HALF], U8, name="vg_bytes%d" % i, align_bytes=64) for i in range(2)]
        c = [psum.tile([P, HALF], F32, name="c%d" % i) for i in range(2)]
        for i in range(2):
            nc.vector.tensor_copy(vg_bytes[i][:], v_bytes[:].indirect(offsets[:, list_halves[i]]))
            nc.tensor.matmul_mx(out=c[i][:], lhsT=g_codes[:].bitcast(FP8X4), lhsT_scale=g_scales[:],
                                rhs=vg_words[:, halves[i]].bitcast(FP4X4), rhs_scale=vg_bytes[i][:],
                                start=True, stop=True)

        t = keep.tile([P, SLOTS], F32, name="t", tag="g_raw")
        e = wide("e")
        t2 = wide("t2")
        y = wide("y")
        r2 = wide("r2")
        for i in range(2):
            cols = halves[i]
            nc.scalar.activation(out=t[:, cols], in_=scores[i][:], func=ACT.Tanh, scale=0.5, accum_out=sums[:, 2 + i : 3 + i])
            nc.scalar.activation(out=e[:, cols], in_=scores[i][:], func=ACT.Exp, accum_out=sums[:, i : i + 1])
        for cols in halves:
            nc.scalar.activation(out=t2[:, cols], in_=t[:, cols], func=ACT.Square)
        for cols in halves:
            nc.scalar.activation(out=y[:, cols], in_=t2[:, cols], func=ACT.Identity, scale=neg_gamma[:], bias=gamma[:])
        nc.scalar.activation(out=r2[:], in_=t[:], func=ACT.Square, bias=1.0)

        z = column("z")
        rz = column("rz")
        reuse = keep.tile([P, 2 * SLOTS + 8], F32, name="reuse", tag="vb")
        g = reuse[:, 0:SLOTS]
        d = reuse[:, SLOTS : 2 * SLOTS]
        terms = reuse[:, 2 * SLOTS : 2 * SLOTS + 5]
        nc.vector.scalar_tensor_tensor(terms, sums[:], 1.0, weights[:], ALU.mult, ALU.mult, accum_out=z[:])
        nc.vector.scalar_tensor_tensor(g[:, halves[0]], e[:, halves[0]], share_sb[:], y[:, halves[0]], ALU.mult, ALU.add)
        nc.vector.reciprocal(rz[:], z[:])
        nc.vector.scalar_tensor_tensor(d[:, halves[0]], t[:, halves[0]], 1.0, y[:, halves[0]], ALU.add, ALU.mult)
        nc.vector.scalar_tensor_tensor(g[:, halves[1]], e[:, halves[1]], share_sb[:], y[:, halves[1]], ALU.mult, ALU.add)
        nc.vector.scalar_tensor_tensor(d[:, halves[1]], t[:, halves[1]], 1.0, y[:, halves[1]], ALU.add, ALU.mult)
        h = wide("h")
        nc.gpsimd.tensor_tensor(h[:], g, d, ALU.subtract)

        parts = keep.tile([P, 4], F32, name="parts")
        c_g = wide("c_g")
        c_r2 = wide("c_r2")
        for i, cols in enumerate(halves):
            nc.vector.scalar_tensor_tensor(c_g[:, cols], c[i][:], -1.0, g[:, cols], ALU.mult, ALU.mult, accum_out=parts[:, i : i + 1])
        for i, cols in enumerate(halves):
            nc.vector.scalar_tensor_tensor(c_r2[:, cols], c[i][:], neg_gamma[:], r2[:, cols], ALU.mult, ALU.mult, accum_out=parts[:, 2 + i : 3 + i])

        g2 = wide("g2")
        m0 = column("m0")
        nc.scalar.activation(out=g2[:], in_=g, func=ACT.Square, scale=rz[:], accum_out=m0[:])
        c_g2 = wide("c_g2")
        a_terms = keep.tile([P, 3], F32, name="a_terms")
        for i, cols in enumerate(halves):
            nc.vector.scalar_tensor_tensor(c_g2[:, cols], c[i][:], 1.0, g2[:, cols], ALU.mult, ALU.mult, accum_out=a_terms[:, i : i + 1])
        k_rz = column("k_rz")
        nc.scalar.mul(k_rz[:], rz[:], PENALTY)
        c2_g2 = wide("c2_g2")
        m2 = column("m2")
        nc.scalar.activation(out=c2_g2[:], in_=c_g[:], func=ACT.Square, scale=rz[:], accum_out=m2[:])
        neg_m = column("neg_m")
        parts_rz = keep.tile([P, 4], F32, name="parts_rz")
        nc.scalar.activation(out=parts_rz[:], in_=parts[:], func=ACT.Identity, scale=rz[:], accum_out=neg_m[:])
        u = wide("u")
        nc.scalar.activation(out=u[:, halves[0]], in_=c[0][:], func=ACT.Identity, bias=neg_m[:])
        nc.scalar.activation(out=a_terms[:, 2:3], in_=m0[:], func=ACT.Identity, scale=neg_m[:])
        nc.scalar.activation(out=u[:, halves[1]], in_=c[1][:], func=ACT.Identity, bias=neg_m[:])
        sum_a = column("sum_a")
        a_copy = keep.tile([P, 3], F32, name="a_copy")
        nc.scalar.activation(out=a_copy[:], in_=a_terms[:], func=ACT.Identity, accum_out=sum_a[:])
        m_m0 = column("m_m0")
        nc.scalar.mul(m_m0[:], a_terms[:, 2:3], -1.0)
        inner = column("inner")
        nc.scalar.activation(out=inner[:], in_=sum_a[:], func=ACT.Identity, scale=2.0, bias=m_m0[:])
        sum_b = column("sum_b")
        nc.scalar.activation(out=sum_b[:], in_=inner[:], func=ACT.Identity, scale=neg_m[:], bias=m2[:])

        x1 = wide("x1")
        x2 = wide("x2")
        x3 = wide("x3")
        result = wide("result")
        for cols in halves:
            nc.vector.scalar_tensor_tensor(x1[:, cols], u[:, cols], rz[:], h[:, cols], ALU.mult, ALU.mult)
        for cols in halves:
            nc.vector.scalar_tensor_tensor(x2[:, cols], x1[:, cols], sum_a[:], u[:, cols], ALU.subtract, ALU.mult)
        for cols in halves:
            nc.vector.scalar_tensor_tensor(x3[:, cols], x2[:, cols], sum_b[:], g[:, cols], ALU.subtract, ALU.mult)
        for cols, queue in zip(halves, (nc.sync, nc.scalar)):
            nc.vector.scalar_tensor_tensor(result[:, cols], x3[:, cols], k_rz[:], base_sb[:, cols], ALU.mult, ALU.add)
            queue.dma_start(out=out[:, cols], in_=result[:, cols])
